import numpy as np
import ml_dtypes


def mxq(x, axis, fmt="e4m3"):
    dtype, down = {"e4m3": (ml_dtypes.float8_e4m3fn, 7), "e5m2": (ml_dtypes.float8_e5m2, 14)}[fmt]
    v = np.moveaxis(np.asarray(x, np.float32).astype(ml_dtypes.bfloat16).astype(np.float64), axis, -1)
    blocks = v.reshape(v.shape[:-1] + (-1, 32))
    amax = np.abs(blocks).max(-1, keepdims=True)
    byte = np.maximum(np.where(amax > 0, np.frexp(amax)[1] - 1 + 127, 0) - down, 1)
    scale = np.exp2(byte - 127.0)
    codes = (blocks / scale).astype(np.float32).astype(dtype).astype(np.float64)
    return np.moveaxis((codes * scale).reshape(v.shape), -1, axis)


WIDE = False


def mx_kscale(k):
    if not WIDE:
        return np.ones(k)
    levels = np.array([10, -10, 5, -5, 0])
    if k % 512:
        return np.exp2(np.random.permutation(np.resize(levels, k // 32))).repeat(32)
    a = np.empty((k // 512, 16))
    for p in range(k // 512):
        a[p, :8] = np.random.permutation(np.resize(levels, 8))
        for g in range(8):
            far = levels[np.abs(levels - a[p, g]) >= 10]
            a[p, g + 8] = far[np.random.randint(len(far))]
    return np.exp2(a.ravel()).repeat(32)


def f64(x):
    return np.asarray(x).astype(np.float64)


def striped(idx):
    return np.tile(idx.reshape(-1, 16).T, (8, 1)).astype(np.uint16)


def unstriped(offs):
    return offs[:16].T.reshape(-1).astype(np.int64)


def pack_weight(w):
    k, n = w.shape
    w = f64(np.asarray(w, np.float32).astype(ml_dtypes.bfloat16)).reshape(k // 32, 32, n)
    amax = np.abs(w).max(1)
    byte = np.clip(np.where(amax > 0, np.frexp(amax)[1] - 1 + 127 - 7, 1), 1, 254)
    scaled = (w * np.exp2(127.0 - byte)[:, None, :]).reshape(k, n).astype(np.float32)
    words = np.ascontiguousarray(scaled.reshape(k // 512, 128, 4, n).transpose(0, 1, 3, 2)).astype(ml_dtypes.float8_e4m3fn).view(np.uint8)
    return words, np.ascontiguousarray(byte.astype(np.uint8).reshape(k // 512, 16, n))


def unpack_weight(words, scales):
    g, p, n, _ = words.shape
    vals = np.ascontiguousarray(words).view(ml_dtypes.float8_e4m3fn).astype(np.float64) * np.repeat(np.exp2(scales.astype(np.float64) - 127.0), 8, axis=1)[..., None]
    return vals.transpose(0, 1, 3, 2).reshape(g * 512, n)


def relu(v):
    return np.maximum(v, 0.0)


K, T, S, W, V, H, G = 512, 1024, 512, 1024, 512, 512, 2048


def setup_inputs():
    n = np.random.standard_normal
    s = mx_kscale(K)[:, None]
    u = mx_kscale(H)
    packed_xT = pack_weight(n((K, T)) * s)
    packed_eT = pack_weight(n((K, W)) * s)
    packed_vT = pack_weight(n((H, G)) / np.sqrt(H) / u[:, None])
    return {
        "x_words": packed_xT[0],
        "x_scales": packed_xT[1],
        "e_words": packed_eT[0],
        "e_scales": packed_eT[1],
        "w1": (n((K, H)) / np.sqrt(2 * K) / s * u).astype(np.float32),
        "w2": (n((K, H)) / np.sqrt(2 * K) / s * u).astype(np.float32),
        "v_words": packed_vT[0],
        "v_scales": packed_vT[1],
        "offs": striped(np.random.permutation(T)[:S]),
        "tok": striped(np.random.permutation(W)[:S]),
        "cand": striped(np.random.permutation(G)[:V]),
    }


def reference(x_words, x_scales, e_words, e_scales, w1, w2, v_words, v_scales, offs, tok, cand):
    xq = unpack_weight(x_words, x_scales)[:, unstriped(offs)]
    e_tok = unpack_weight(e_words, e_scales)[:, unstriped(tok)]
    h = relu(mxq(f64(w1), 0, "e4m3").T @ xq + mxq(f64(w2), 0, "e4m3").T @ e_tok)
    v_cand = unpack_weight(v_words, v_scales)[:, unstriped(cand)]
    y = mxq(h, 0, "e4m3").T @ v_cand
    e = np.exp(y - y.max(axis=1, keepdims=True))
    return e / e.sum(axis=1, keepdims=True)

@@ -1,0 +1,152 @@
+from contextlib import ExitStack
+
+import concourse.mybir as mybir
+
+F32 = mybir.dt.float32
+BF16 = mybir.dt.bfloat16
+I32 = mybir.dt.int32
+U32 = mybir.dt.uint32
+U16 = mybir.dt.uint16
+U8 = mybir.dt.uint8
+FP8X4 = mybir.dt.float8_e4m3fn_x4
+ACT = mybir.ActivationFunctionType
+ALU = mybir.AluOpType
+AX = mybir.AxisListType
+
+P = 128
+PACK = 4
+K = 512
+H = 512
+S = 512
+V = 512
+CH = 128
+FLOPS = 2 * (2 * K * H * S + H * S * V)
+
+
+def tile_picked_zfrs_relu_p_kernel(tc, x_words, x_scales, e_words, e_scales, w1, w2, v_words, v_scales, offs, tok, cand, out):
+    nc = tc.nc
+    with ExitStack() as ctx:
+        keep = ctx.enter_context(tc.tile_pool(name="keep", bufs=1))
+        psum = ctx.enter_context(tc.psum_pool(name="psum", bufs=1))
+
+        def tile(shape, dtype, name):
+            return keep.tile(shape, dtype, name=name, align_bytes=64)
+
+        def load_list(src, name):
+            t = keep.tile([P, src.shape[1]], U16, name=name)
+            nc.sync.dma_start(t[:], src)
+            return t
+
+        def clear_scales(src, name, eng):
+            t = tile([P, src.shape[2]], U8, name)
+            eng.memset(t[:].bitcast(I32), 0)
+            return t
+
+        def load_scales(t, src):
+            nc.sync.dma_start(t[0:16, :].bitcast(I32), src[0].bitcast(I32))
+
+        def load_words(src, name):
+            t = tile([P, src.shape[2]], I32, name)
+            nc.sync.dma_start(t[:], src[0].rearrange("p n t -> p (n t)").bitcast(I32))
+            return t
+
+        def load_w(src, half, name):
+            t = tile([P, PACK, H // 2], F32, name)
+            nc.sync.dma_start(t[:], src.rearrange("(p j) c -> p j c", j=PACK)[:, :, half * (H // 2) : (half + 1) * (H // 2)])
+            return t
+
+        def cast_w(grouped, raw, half, eng):
+            m0 = half * (P // 2)
+            dst = grouped[:].rearrange("p (t m j) -> p m j t", t=PACK, j=PACK)[:, m0 : m0 + P // 2]
+            src = raw[:].rearrange("p j (m t) -> p m j t", t=PACK)
+            if eng is nc.scalar:
+                nc.scalar.copy(dst, src)
+            else:
+                nc.vector.tensor_copy(dst, src)
+
+        def quantise(grouped, width, name):
+            codes = tile([P, width], U32, name + "_codes")
+            scales = tile([P, width], U8, name + "_scales")
+            nc.vector.quantize_mx(out=codes[:].bitcast(FP8X4), scales=scales[:], in_=grouped[:])
+            return codes, scales
+
+        def gather(window, offsets, dtype, name):
+            t = tile([P, 16 * offsets.shape[1]], dtype, name)
+            nc.vector.tensor_copy(t[:], window.indirect(offsets))
+            return t
+
+        xs_win = clear_scales(x_scales, "xs_win", nc.gpsimd)
+        es_win = clear_scales(e_scales, "es_win", nc.vector)
+        vs_win = clear_scales(v_scales, "vs_win", nc.vector)
+        planes = tile([P, 3 * S], U8, "planes")
+        nc.gpsimd.memset(planes[:].bitcast(I32), 0)
+        warm = tile([P, 1], F32, "warm")
+        warm_out = tile([P, 1], F32, "warm_out")
+        nc.gpsimd.memset(warm[:], 0.0)
+        nc.scalar.activation(warm_out[:], warm[:], ACT.Exp)
+
+        offs_t = load_list(offs, "offs_t")
+        load_scales(xs_win, x_scales)
+        tok_t = load_list(tok, "tok_t")
+        load_scales(es_win, e_scales)
+        w1a = load_w(w1, 0, "w1a")
+        cand_t = load_list(cand, "cand_t")
+        load_scales(vs_win, v_scales)
+        w1b = load_w(w1, 1, "w1b")
+        x_win = load_words(x_words, "x_win")
+        w2a = load_w(w2, 0, "w2a")
+        w2b = load_w(w2, 1, "w2b")
+        e_win = load_words(e_words, "e_win")
+
+        g1 = tile([P, PACK * H], BF16, "g1")
+        g2 = tile([P, PACK * H], BF16, "g2")
+        picked = tile([P, 3 * S], U8, "picked")
+        nc.vector.tensor_copy(picked[:, 0:S], xs_win[:].indirect(offs_t[:]))
+        cast_w(g1, w1a, 0, nc.scalar)
+        nc.vector.tensor_copy(picked[:, S : 2 * S], es_win[:].indirect(tok_t[:]))
+        cast_w(g1, w1b, 1, nc.scalar)
+        nc.vector.tensor_copy(picked[:, 2 * S : 3 * S], vs_win[:].indirect(cand_t[:]))
+        for q in range(4):
+            nc.sync.dma_start(planes[32 * q : 32 * q + 4, :].bitcast(I32), picked[4 * q : 4 * q + 4, :].bitcast(I32))
+        v_win = load_words(v_words, "v_win")
+        xs, es, vs = planes[:, 0:S], planes[:, S : 2 * S], planes[:, 2 * S : 3 * S]
+        xg = gather(x_win[:].bitcast(U32), offs_t[:], U32, "xg")
+        cast_w(g2, w2a, 0, nc.scalar)
+        w1c, w1s = quantise(g1, H, "w1")
+        cast_w(g2, w2b, 1, nc.vector)
+        w2c, w2s = quantise(g2, H, "w2")
+        eg0 = gather(e_win[:].bitcast(U32), tok_t[:, 0 : CH // 16], U32, "eg0")
+        eg1 = gather(e_win[:].bitcast(U32), tok_t[:, CH // 16 :], U32, "eg1")
+        vg = gather(v_win[:].bitcast(U32), cand_t[:], U32, "vg")
+
+        n_ch = S // CH
+        hq = []
+        for c in range(n_ch):
+            cols = slice(c * CH, (c + 1) * CH)
+            e_cols = eg0[:] if c == 0 else eg1[:, (c - 1) * CH : c * CH]
+            hp = psum.tile([P, PACK, CH], F32, name=f"hp{c}")
+            for t in range(PACK):
+                wc = slice(t * P, (t + 1) * P)
+                nc.tensor.matmul_mx(out=hp[:, t, :], lhsT=w1c[:, wc].bitcast(FP8X4), lhsT_scale=w1s[:, wc],
+                                    rhs=xg[:, cols].bitcast(FP8X4), rhs_scale=xs[:, cols], start=True, stop=False)
+                nc.tensor.matmul_mx(out=hp[:, t, :], lhsT=w2c[:, wc].bitcast(FP8X4), lhsT_scale=w2s[:, wc],
+                                    rhs=e_cols.bitcast(FP8X4), rhs_scale=es[:, cols], start=False, stop=True)
+            hb = tile([P, CH * PACK], BF16, f"hb{c}")
+            nc.scalar.activation(hb[:].rearrange("p (n t) -> p n t", t=PACK), hp[:].rearrange("p t n -> p n t"), ACT.Relu)
+            hq.append(quantise(hb, CH, f"h{c}"))
+
+        for c in range(n_ch):
+            hc, hs = hq[c]
+            yp = psum.tile([P, V], F32, name=f"yp{c}")
+            nc.tensor.matmul_mx(out=yp[:], lhsT=hc[:].bitcast(FP8X4), lhsT_scale=hs[:],
+                                rhs=vg[:].bitcast(FP8X4), rhs_scale=vs, start=True, stop=True)
+            negmax = tile([P, 1], F32, f"negmax{c}")
+            nc.vector.tensor_reduce(negmax[:], yp[:], AX.X, ALU.max, negate=True)
+            ex = tile([P, V], F32, f"ex{c}")
+            total = tile([P, 1], F32, f"total{c}")
+            nc.scalar.activation(ex[:], yp[:], ACT.Exp, bias=negmax[:], scale=1.0, accum_out=total[:])
+            inv = tile([P, 1], F32, f"inv{c}")
+            nc.vector.reciprocal(inv[:], total[:])
+            res = tile([P, V], F32, f"res{c}")
+            nc.vector.tensor_scalar(res[:], ex[:], inv[:], None, ALU.mult)
+            nc.sync.dma_start(out[c * CH : (c + 1) * CH, :], res[:])

@@ -50,15 +50,14 @@ def tile_picked_zfrs_relu_p_kernel(tc, x_words, x_scales, e_words, e_scales, w1,
             nc.sync.dma_start(t[:], src[0].rearrange("p n t -> p (n t)").bitcast(I32))
             return t
 
-        def load_w(src, half, name):
-            t = tile([P, PACK, H // 2], F32, name)
-            nc.sync.dma_start(t[:], src.rearrange("(p j) c -> p j c", j=PACK)[:, :, half * (H // 2) : (half + 1) * (H // 2)])
+        def load_w(src, name):
+            t = tile([P, PACK, H], F32, name)
+            nc.sync.dma_start(t[:], src.rearrange("(p j) c -> p j c", j=PACK))
             return t
 
-        def cast_w(grouped, raw, half, eng):
-            m0 = half * (P // 2)
-            dst = grouped[:].rearrange("p (t m j) -> p m j t", t=PACK, j=PACK)[:, m0 : m0 + P // 2]
-            src = raw[:].rearrange("p j (m t) -> p m j t", t=PACK)
+        def cast_w(grouped, raw, lo, hi, eng):
+            dst = grouped[:].rearrange("p (t m j) -> p m j t", t=PACK, j=PACK)[:, lo:hi]
+            src = raw[:].rearrange("p j (m t) -> p m j t", t=PACK)[:, lo:hi]
             if eng is nc.scalar:
                 nc.scalar.copy(dst, src)
             else:
@@ -78,75 +77,118 @@ def tile_picked_zfrs_relu_p_kernel(tc, x_words, x_scales, e_words, e_scales, w1,
         xs_win = clear_scales(x_scales, "xs_win", nc.gpsimd)
         es_win = clear_scales(e_scales, "es_win", nc.vector)
         vs_win = clear_scales(v_scales, "vs_win", nc.vector)
-        planes = tile([P, 3 * S], U8, "planes")
+        planes = tile([P, 2 * S], U8, "planes")
         nc.gpsimd.memset(planes[:].bitcast(I32), 0)
+        v_plane = tile([P, V], U8, "v_plane")
+        nc.gpsimd.memset(v_plane[:].bitcast(I32), 0)
         warm = tile([P, 1], F32, "warm")
         warm_out = tile([P, 1], F32, "warm_out")
         nc.gpsimd.memset(warm[:], 0.0)
-        nc.scalar.activation(warm_out[:], warm[:], ACT.Exp)
 
         offs_t = load_list(offs, "offs_t")
         load_scales(xs_win, x_scales)
+        nc.scalar.activation(warm_out[:], warm[:], ACT.Exp)
         tok_t = load_list(tok, "tok_t")
         load_scales(es_win, e_scales)
-        w1a = load_w(w1, 0, "w1a")
+        w1_raw = load_w(w1, "w1_raw")
         cand_t = load_list(cand, "cand_t")
         load_scales(vs_win, v_scales)
-        w1b = load_w(w1, 1, "w1b")
+        w2_raw = load_w(w2, "w2_raw")
         x_win = load_words(x_words, "x_win")
-        w2a = load_w(w2, 0, "w2a")
-        w2b = load_w(w2, 1, "w2b")
-        e_win = load_words(e_words, "e_win")
+
+        def place(dst, src):
+            for q in range(4):
+                nc.sync.dma_start(dst[32 * q : 32 * q + 4, :].bitcast(I32), src[4 * q : 4 * q + 4, :].bitcast(I32))
 
         g1 = tile([P, PACK * H], BF16, "g1")
         g2 = tile([P, PACK * H], BF16, "g2")
-        picked = tile([P, 3 * S], U8, "picked")
+        picked = tile([P, 2 * S], U8, "picked")
+        v_picked = tile([P, V], U8, "v_picked")
         nc.vector.tensor_copy(picked[:, 0:S], xs_win[:].indirect(offs_t[:]))
-        cast_w(g1, w1a, 0, nc.scalar)
         nc.vector.tensor_copy(picked[:, S : 2 * S], es_win[:].indirect(tok_t[:]))
-        cast_w(g1, w1b, 1, nc.scalar)
-        nc.vector.tensor_copy(picked[:, 2 * S : 3 * S], vs_win[:].indirect(cand_t[:]))
-        for q in range(4):
-            nc.sync.dma_start(planes[32 * q : 32 * q + 4, :].bitcast(I32), picked[4 * q : 4 * q + 4, :].bitcast(I32))
+        place(planes, picked)
+        e_win = load_words(e_words, "e_win")
         v_win = load_words(v_words, "v_win")
-        xs, es, vs = planes[:, 0:S], planes[:, S : 2 * S], planes[:, 2 * S : 3 * S]
-        xg = gather(x_win[:].bitcast(U32), offs_t[:], U32, "xg")
-        cast_w(g2, w2a, 0, nc.scalar)
+        cast_w(g1, w1_raw, 0, 80, nc.scalar)
+        nc.vector.tensor_copy(v_picked[:], vs_win[:].indirect(cand_t[:]))
+        place(v_plane, v_picked)
+        xs, es, vs = planes[:, 0:S], planes[:, S : 2 * S], v_plane[:]
+        cast_w(g1, w1_raw, 80, 128, nc.vector)
         w1c, w1s = quantise(g1, H, "w1")
-        cast_w(g2, w2b, 1, nc.vector)
+        cast_w(g2, w2_raw, 0, 64, nc.scalar)
+        cast_w(g2, w2_raw, 64, 128, nc.vector)
+        xg_all = gather(x_win[:].bitcast(U32), offs_t[:], U32, "xg")
         w2c, w2s = quantise(g2, H, "w2")
-        eg0 = gather(e_win[:].bitcast(U32), tok_t[:, 0 : CH // 16], U32, "eg0")
-        eg1 = gather(e_win[:].bitcast(U32), tok_t[:, CH // 16 :], U32, "eg1")
-        vg = gather(v_win[:].bitcast(U32), cand_t[:], U32, "vg")
-
         n_ch = S // CH
-        hq = []
+        eg0 = gather(e_win[:].bitcast(U32), tok_t[:, 0 : CH // 16], U32, "eg0")
+        eg1 = gather(e_win[:].bitcast(U32), tok_t[:, CH // 16 : 2 * CH // 16], U32, "eg1")
+        eg2 = gather(e_win[:].bitcast(U32), tok_t[:, 2 * CH // 16 :], U32, "eg2")
+        xg = [xg_all[:, c * CH : (c + 1) * CH] for c in range(n_ch)]
+        eg = [eg0[:], eg1[:], eg2[:, 0:CH], eg2[:, CH:]]
+
+        yp = [psum.tile([P, V], F32, name=f"yp{c}") for c in range(n_ch)]
+        for c in range(3):
+            nc.tensor.matmul_mx(out=yp[c][:], lhsT=w1c[:, 0:P].bitcast(FP8X4), lhsT_scale=w1s[:, 0:P],
+                                rhs=w1c[:].bitcast(FP8X4), rhs_scale=w1s[:], start=True, stop=True)
+        hb = []
         for c in range(n_ch):
             cols = slice(c * CH, (c + 1) * CH)
-            e_cols = eg0[:] if c == 0 else eg1[:, (c - 1) * CH : c * CH]
             hp = psum.tile([P, PACK, CH], F32, name=f"hp{c}")
             for t in range(PACK):
                 wc = slice(t * P, (t + 1) * P)
                 nc.tensor.matmul_mx(out=hp[:, t, :], lhsT=w1c[:, wc].bitcast(FP8X4), lhsT_scale=w1s[:, wc],
-                                    rhs=xg[:, cols].bitcast(FP8X4), rhs_scale=xs[:, cols], start=True, stop=False)
+                                    rhs=xg[c].bitcast(FP8X4), rhs_scale=xs[:, cols], start=True, stop=False)
                 nc.tensor.matmul_mx(out=hp[:, t, :], lhsT=w2c[:, wc].bitcast(FP8X4), lhsT_scale=w2s[:, wc],
-                                    rhs=e_cols.bitcast(FP8X4), rhs_scale=es[:, cols], start=False, stop=True)
-            hb = tile([P, CH * PACK], BF16, f"hb{c}")
-            nc.scalar.activation(hb[:].rearrange("p (n t) -> p n t", t=PACK), hp[:].rearrange("p t n -> p n t"), ACT.Relu)
-            hq.append(quantise(hb, CH, f"h{c}"))
+                                    rhs=eg[c].bitcast(FP8X4), rhs_scale=es[:, cols], start=False, stop=True)
+            hb.append(tile([P, CH * PACK], BF16, f"hb{c}"))
+            nc.scalar.activation(hb[c][:].rearrange("p (n t) -> p n t", t=PACK), hp[:].rearrange("p t n -> p n t"), ACT.Relu)
 
+        HV = V // 2
+        vg = [gather(v_win[:].bitcast(U32), cand_t[:, u * HV // 16 : (u + 1) * HV // 16], U32, f"vg{u}") for u in range(2)]
+        h_codes = keep.tile([P, S], U32, name="h_codes", tag="v_win", align_bytes=64)
+        hq = []
         for c in range(n_ch):
+            cols = slice(c * CH, (c + 1) * CH)
+            h_scales = tile([P, CH], U8, f"h_scales{c}")
+            nc.vector.quantize_mx(out=h_codes[:, cols].bitcast(FP8X4), scales=h_scales[:], in_=hb[c][:])
+            hq.append((h_codes[:, cols], h_scales[:]))
+
+        ex = [tile([P, V], F32, f"ex{c}") for c in range(n_ch)]
+        total = [tile([P, 1], F32, f"total{c}") for c in range(n_ch)]
+        inv = [tile([P, 1], F32, f"inv{c}") for c in range(n_ch)]
+
+        def logits(c):
             hc, hs = hq[c]
-            yp = psum.tile([P, V], F32, name=f"yp{c}")
-            nc.tensor.matmul_mx(out=yp[:], lhsT=hc[:].bitcast(FP8X4), lhsT_scale=hs[:],
-                                rhs=vg[:].bitcast(FP8X4), rhs_scale=vs, start=True, stop=True)
+            for u in range(2):
+                vc = slice(u * HV, (u + 1) * HV)
+                nc.tensor.matmul_mx(out=yp[c][:, vc], lhsT=hc.bitcast(FP8X4), lhsT_scale=hs,
+                                    rhs=vg[u][:].bitcast(FP8X4), rhs_scale=vs[:, vc], start=True, stop=True)
             negmax = tile([P, 1], F32, f"negmax{c}")
-            nc.vector.tensor_reduce(negmax[:], yp[:], AX.X, ALU.max, negate=True)
-            ex = tile([P, V], F32, f"ex{c}")
-            total = tile([P, 1], F32, f"total{c}")
-            nc.scalar.activation(ex[:], yp[:], ACT.Exp, bias=negmax[:], scale=1.0, accum_out=total[:])
-            inv = tile([P, 1], F32, f"inv{c}")
-            nc.vector.reciprocal(inv[:], total[:])
+            nc.vector.tensor_reduce(negmax[:], yp[c][:], AX.X, ALU.max, negate=True)
+            nc.scalar.activation(ex[c][:], yp[c][:], ACT.Exp, bias=negmax[:], scale=1.0, accum_out=total[c][:])
+
+        def invert(c):
+            nc.vector.reciprocal(inv[c][:], total[c][:])
+
+        def finish(c):
             res = tile([P, V], F32, f"res{c}")
-            nc.vector.tensor_scalar(res[:], ex[:], inv[:], None, ALU.mult)
+            nc.vector.tensor_scalar(res[:], ex[c][:], inv[c][:], None, ALU.mult)
             nc.sync.dma_start(out[c * CH : (c + 1) * CH, :], res[:])
+
+        logits(0)
+        logits(1)
+        logits(2)
+        invert(0)
+        logits(3)
+        invert(1)
+        finish(0)
+        finish(1)
+        invert(2)
+        finish(2)
+        invert(3)
+        res_a = tile([P, HV], F32, "res_a")
+        res_b = tile([P, HV], F32, "res_b")
+        nc.vector.tensor_scalar(res_a[:], ex[3][:, 0:HV], inv[3][:], None, ALU.mult)
+        nc.sync.dma_start(out[3 * CH :, 0:HV], res_a[:])
+        nc.scalar.activation(res_b[:], ex[3][:, HV:], ACT.Copy, scale=inv[3][:])
+        nc.scalar.dma_start(out[3 * CH :, HV:], res_b[:])

@@ -43,7 +43,7 @@ def tile_picked_zfrs_relu_p_kernel(tc, x_words, x_scales, e_words, e_scales, w1,
             return t
 
         def load_scales(t, src):
-            nc.sync.dma_start(t[0:16, :].bitcast(I32), src[0].bitcast(I32))
+            nc.sync.dma_start(t[0:P:8, :].bitcast(I32), src[0].bitcast(I32))
 
         def load_words(src, name):
             t = tile([P, src.shape[2]], I32, name)
@@ -97,8 +97,8 @@ def tile_picked_zfrs_relu_p_kernel(tc, x_words, x_scales, e_words, e_scales, w1,
         x_win = load_words(x_words, "x_win")
 
         def place(dst, src):
-            for q in range(4):
-                nc.sync.dma_start(dst[32 * q : 32 * q + 4, :].bitcast(I32), src[4 * q : 4 * q + 4, :].bitcast(I32))
+            for r in range(4):
+                nc.sync.dma_start(dst[r:P:32, :].bitcast(I32), src[8 * r : P : 32, :].bitcast(I32))
 
         g1 = tile([P, PACK * H], BF16, "g1")
         g2 = tile([P, PACK * H], BF16, "g2")
@@ -117,13 +117,13 @@ def tile_picked_zfrs_relu_p_kernel(tc, x_words, x_scales, e_words, e_scales, w1,
         w1c, w1s = quantise(g1, H, "w1")
         cast_w(g2, w2_raw, 0, 64, nc.scalar)
         cast_w(g2, w2_raw, 64, 128, nc.vector)
-        xg_all = gather(x_win[:].bitcast(U32), offs_t[:], U32, "xg")
+        xg_a = gather(x_win[:].bitcast(U32), offs_t[:, 0 : 2 * CH // 16], U32, "xg_a")
         w2c, w2s = quantise(g2, H, "w2")
         n_ch = S // CH
         eg0 = gather(e_win[:].bitcast(U32), tok_t[:, 0 : CH // 16], U32, "eg0")
         eg1 = gather(e_win[:].bitcast(U32), tok_t[:, CH // 16 : 2 * CH // 16], U32, "eg1")
         eg2 = gather(e_win[:].bitcast(U32), tok_t[:, 2 * CH // 16 :], U32, "eg2")
-        xg = [xg_all[:, c * CH : (c + 1) * CH] for c in range(n_ch)]
+        xg = [xg_a[:, 0:CH], xg_a[:, CH:]]
         eg = [eg0[:], eg1[:], eg2[:, 0:CH], eg2[:, CH:]]
 
         yp = [psum.tile([P, V], F32, name=f"yp{c}") for c in range(n_ch)]
@@ -133,6 +133,11 @@ def tile_picked_zfrs_relu_p_kernel(tc, x_words, x_scales, e_words, e_scales, w1,
         hb = []
         for c in range(n_ch):
             cols = slice(c * CH, (c + 1) * CH)
+            if c == 2:
+                xg_b = keep.tile([P, 2 * CH], U32, name="xg_b", tag="eg0", align_bytes=64)
+                for b in range(2):
+                    nc.vector.tensor_copy(xg_b[:, b * CH : (b + 1) * CH], x_win[:].bitcast(U32).indirect(offs_t[:, (2 + b) * CH // 16 : (3 + b) * CH // 16]))
+                xg.extend([xg_b[:, 0:CH], xg_b[:, CH:]])
             hp = psum.tile([P, PACK, CH], F32, name=f"hp{c}")
             for t in range(PACK):
                 wc = slice(t * P, (t + 1) * P)
@@ -146,12 +151,18 @@ def tile_picked_zfrs_relu_p_kernel(tc, x_words, x_scales, e_words, e_scales, w1,
         HV = V // 2
         vg = [gather(v_win[:].bitcast(U32), cand_t[:, u * HV // 16 : (u + 1) * HV // 16], U32, f"vg{u}") for u in range(2)]
         h_codes = keep.tile([P, S], U32, name="h_codes", tag="v_win", align_bytes=64)
+        h_first = tile([P, CH], U32, "h_first")
         hq = []
-        for c in range(n_ch):
+
+        def quantise_h(c):
             cols = slice(c * CH, (c + 1) * CH)
             h_scales = tile([P, CH], U8, f"h_scales{c}")
-            nc.vector.quantize_mx(out=h_codes[:, cols].bitcast(FP8X4), scales=h_scales[:], in_=hb[c][:])
-            hq.append((h_codes[:, cols], h_scales[:]))
+            codes = h_first[:] if c == 0 else h_codes[:, cols]
+            nc.vector.quantize_mx(out=codes.bitcast(FP8X4), scales=h_scales[:], in_=hb[c][:])
+            hq.append((codes, h_scales[:]))
+
+        for c in range(3):
+            quantise_h(c)
 
         ex = [tile([P, V], F32, f"ex{c}") for c in range(n_ch)]
         total = [tile([P, 1], F32, f"total{c}") for c in range(n_ch)]
@@ -176,6 +187,7 @@ def tile_picked_zfrs_relu_p_kernel(tc, x_words, x_scales, e_words, e_scales, w1,
             nc.sync.dma_start(out[c * CH : (c + 1) * CH, :], res[:])
 
         logits(0)
+        quantise_h(3)
         logits(1)
         logits(2)
         invert(0)

@@ -75,12 +75,12 @@ def tile_picked_zfrs_relu_p_kernel(tc, x_words, x_scales, e_words, e_scales, w1,
             return t
 
         xs_win = clear_scales(x_scales, "xs_win", nc.gpsimd)
-        es_win = clear_scales(e_scales, "es_win", nc.vector)
+        es_win = clear_scales(e_scales, "es_win", nc.gpsimd)
         vs_win = clear_scales(v_scales, "vs_win", nc.vector)
         planes = tile([P, 2 * S], U8, "planes")
-        nc.gpsimd.memset(planes[:].bitcast(I32), 0)
+        nc.vector.memset(planes[:].bitcast(I32), 0)
         v_plane = tile([P, V], U8, "v_plane")
-        nc.gpsimd.memset(v_plane[:].bitcast(I32), 0)
+        nc.vector.memset(v_plane[:].bitcast(I32), 0)
         warm = tile([P, 1], F32, "warm")
         warm_out = tile([P, 1], F32, "warm_out")
         nc.gpsimd.memset(warm[:], 0.0)
@@ -88,9 +88,12 @@ def tile_picked_zfrs_relu_p_kernel(tc, x_words, x_scales, e_words, e_scales, w1,
         offs_t = load_list(offs, "offs_t")
         load_scales(xs_win, x_scales)
         nc.scalar.activation(warm_out[:], warm[:], ACT.Exp)
+        w1_raw = tile([P, PACK, H], F32, "w1_raw")
+        w1_rows = w1.rearrange("(p j) c -> p j c", j=PACK)
+        nc.sync.dma_start(w1_raw[:, 0:2, :], w1_rows[:, 0:2, :])
         tok_t = load_list(tok, "tok_t")
         load_scales(es_win, e_scales)
-        w1_raw = load_w(w1, "w1_raw")
+        nc.sync.dma_start(w1_raw[:, 2:4, :], w1_rows[:, 2:4, :])
         cand_t = load_list(cand, "cand_t")
         load_scales(vs_win, v_scales)
         w2_raw = load_w(w2, "w2_raw")
@@ -106,8 +109,8 @@ def tile_picked_zfrs_relu_p_kernel(tc, x_words, x_scales, e_words, e_scales, w1,
         v_picked = tile([P, V], U8, "v_picked")
         nc.vector.tensor_copy(picked[:, 0:S], xs_win[:].indirect(offs_t[:]))
         nc.vector.tensor_copy(picked[:, S : 2 * S], es_win[:].indirect(tok_t[:]))
-        place(planes, picked)
         e_win = load_words(e_words, "e_win")
+        place(planes, picked)
         v_win = load_words(v_words, "v_win")
         cast_w(g1, w1_raw, 0, 80, nc.scalar)
         nc.vector.tensor_copy(v_picked[:], vs_win[:].indirect(cand_t[:]))

@@ -85,12 +85,13 @@ def tile_picked_zfrs_relu_p_kernel(tc, x_words, x_scales, e_words, e_scales, w1,
         warm_out = tile([P, 1], F32, "warm_out")
         nc.gpsimd.memset(warm[:], 0.0)
 
+        w1_raw = tile([P, PACK, H], F32, "w1_raw")
+        w1_rows = w1.rearrange("(p j) c -> p j c", j=PACK)
+        nc.sync.dma_start(w1_raw[:, 0:1, :], w1_rows[:, 0:1, :])
         offs_t = load_list(offs, "offs_t")
         load_scales(xs_win, x_scales)
         nc.scalar.activation(warm_out[:], warm[:], ACT.Exp)
-        w1_raw = tile([P, PACK, H], F32, "w1_raw")
-        w1_rows = w1.rearrange("(p j) c -> p j c", j=PACK)
-        nc.sync.dma_start(w1_raw[:, 0:2, :], w1_rows[:, 0:2, :])
+        nc.sync.dma_start(w1_raw[:, 1:2, :], w1_rows[:, 1:2, :])
         tok_t = load_list(tok, "tok_t")
         load_scales(es_win, e_scales)
         nc.sync.dma_start(w1_raw[:, 2:4, :], w1_rows[:, 2:4, :])
@@ -196,14 +197,15 @@ def tile_picked_zfrs_relu_p_kernel(tc, x_words, x_scales, e_words, e_scales, w1,
         invert(0)
         logits(3)
         invert(1)
-        finish(0)
-        finish(1)
+        for u in range(2):
+            half = tile([P, HV], F32, f"res_first{u}")
+            nc.vector.tensor_scalar(half[:], ex[0][:, u * HV : (u + 1) * HV], inv[0][:], None, ALU.mult)
+            nc.sync.dma_start(out[0:CH, u * HV : (u + 1) * HV], half[:])
         invert(2)
+        finish(1)
         finish(2)
         invert(3)
-        res_a = tile([P, HV], F32, "res_a")
-        res_b = tile([P, HV], F32, "res_b")
-        nc.vector.tensor_scalar(res_a[:], ex[3][:, 0:HV], inv[3][:], None, ALU.mult)
-        nc.sync.dma_start(out[3 * CH :, 0:HV], res_a[:])
-        nc.scalar.activation(res_b[:], ex[3][:, HV:], ACT.Copy, scale=inv[3][:])
-        nc.scalar.dma_start(out[3 * CH :, HV:], res_b[:])
+        res_last = tile([P, V], F32, "res_last")
+        nc.vector.tensor_scalar(res_last[:, 0:320], ex[3][:, 0:320], inv[3][:], None, ALU.mult)
+        nc.scalar.activation(res_last[:, 320:], ex[3][:, 320:], ACT.Copy, scale=inv[3][:])
+        nc.sync.dma_start(out[3 * CH :, :], res_last[:])

@@ -74,8 +74,8 @@ def tile_picked_zfrs_relu_p_kernel(tc, x_words, x_scales, e_words, e_scales, w1,
             nc.vector.tensor_copy(t[:], window.indirect(offsets))
             return t
 
-        xs_win = clear_scales(x_scales, "xs_win", nc.gpsimd)
-        es_win = clear_scales(e_scales, "es_win", nc.gpsimd)
+        xs_win = clear_scales(x_scales, "xs_win", nc.vector)
+        es_win = clear_scales(e_scales, "es_win", nc.vector)
         vs_win = clear_scales(v_scales, "vs_win", nc.vector)
         planes = tile([P, 2 * S], U8, "planes")
         nc.vector.memset(planes[:].bitcast(I32), 0)
@@ -83,7 +83,7 @@ def tile_picked_zfrs_relu_p_kernel(tc, x_words, x_scales, e_words, e_scales, w1,
         nc.vector.memset(v_plane[:].bitcast(I32), 0)
         warm = tile([P, 1], F32, "warm")
         warm_out = tile([P, 1], F32, "warm_out")
-        nc.gpsimd.memset(warm[:], 0.0)
+        nc.vector.memset(warm[:], 0.0)
 
         w1_raw = tile([P, PACK, H], F32, "w1_raw")
         w1_rows = w1.rearrange("(p j) c -> p j c", j=PACK)

@@ -160,7 +160,7 @@ def tile_picked_zfrs_relu_p_kernel(tc, x_words, x_scales, e_words, e_scales, w1,
 
         def quantise_h(c):
             cols = slice(c * CH, (c + 1) * CH)
-            h_scales = tile([P, CH], U8, f"h_scales{c}")
+            h_scales = keep.tile([P, CH], U8, name=f"h_scales{c}", tag=f"h_scales{c % 3}", align_bytes=64)
             codes = h_first[:] if c == 0 else h_codes[:, cols]
             nc.vector.quantize_mx(out=codes.bitcast(FP8X4), scales=h_scales[:], in_=hb[c][:])
             hq.append((codes, h_scales[:]))

@@ -78,7 +78,6 @@ def tile_picked_zfrs_relu_p_kernel(tc, x_words, x_scales, e_words, e_scales, w1,
         es_win = clear_scales(e_scales, "es_win", nc.vector)
         vs_win = clear_scales(v_scales, "vs_win", nc.vector)
         planes = tile([P, 2 * S], U8, "planes")
-        nc.vector.memset(planes[:].bitcast(I32), 0)
         v_plane = tile([P, V], U8, "v_plane")
         nc.vector.memset(v_plane[:].bitcast(I32), 0)
         warm = tile([P, 1], F32, "warm")
@@ -100,8 +99,8 @@ def tile_picked_zfrs_relu_p_kernel(tc, x_words, x_scales, e_words, e_scales, w1,
         w2_raw = load_w(w2, "w2_raw")
         x_win = load_words(x_words, "x_win")
 
-        def place(dst, src):
-            for r in range(4):
+        def place(dst, src, first):
+            for r in range(first, 4):
                 nc.sync.dma_start(dst[r:P:32, :].bitcast(I32), src[8 * r : P : 32, :].bitcast(I32))
 
         g1 = tile([P, PACK * H], BF16, "g1")
@@ -111,13 +110,14 @@ def tile_picked_zfrs_relu_p_kernel(tc, x_words, x_scales, e_words, e_scales, w1,
         nc.vector.tensor_copy(picked[:, 0:S], xs_win[:].indirect(offs_t[:]))
         nc.vector.tensor_copy(picked[:, S : 2 * S], es_win[:].indirect(tok_t[:]))
         e_win = load_words(e_words, "e_win")
-        place(planes, picked)
+        nc.vector.tensor_copy(planes[:].bitcast(I32), picked[:].bitcast(I32))
+        place(planes, picked, 1)
         v_win = load_words(v_words, "v_win")
-        cast_w(g1, w1_raw, 0, 80, nc.scalar)
+        cast_w(g1, w1_raw, 0, 96, nc.scalar)
         nc.vector.tensor_copy(v_picked[:], vs_win[:].indirect(cand_t[:]))
-        place(v_plane, v_picked)
+        place(v_plane, v_picked, 0)
         xs, es, vs = planes[:, 0:S], planes[:, S : 2 * S], v_plane[:]
-        cast_w(g1, w1_raw, 80, 128, nc.vector)
+        cast_w(g1, w1_raw, 96, 128, nc.vector)
         w1c, w1s = quantise(g1, H, "w1")
         cast_w(g2, w2_raw, 0, 64, nc.scalar)
         cast_w(g2, w2_raw, 64, 128, nc.vector)

@@ -79,6 +79,7 @@ def tile_picked_zfrs_relu_p_kernel(tc, x_words, x_scales, e_words, e_scales, w1,
         vs_win = clear_scales(v_scales, "vs_win", nc.vector)
         planes = tile([P, 2 * S], U8, "planes")
         v_plane = tile([P, V], U8, "v_plane")
+        nc.vector.memset(planes[:].bitcast(I32), 0)
         nc.vector.memset(v_plane[:].bitcast(I32), 0)
         warm = tile([P, 1], F32, "warm")
         warm_out = tile([P, 1], F32, "warm_out")
@@ -109,15 +110,14 @@ def tile_picked_zfrs_relu_p_kernel(tc, x_words, x_scales, e_words, e_scales, w1,
         v_picked = tile([P, V], U8, "v_picked")
         nc.vector.tensor_copy(picked[:, 0:S], xs_win[:].indirect(offs_t[:]))
         nc.vector.tensor_copy(picked[:, S : 2 * S], es_win[:].indirect(tok_t[:]))
+        place(planes, picked, 0)
         e_win = load_words(e_words, "e_win")
-        nc.vector.tensor_copy(planes[:].bitcast(I32), picked[:].bitcast(I32))
-        place(planes, picked, 1)
         v_win = load_words(v_words, "v_win")
-        cast_w(g1, w1_raw, 0, 96, nc.scalar)
+        cast_w(g1, w1_raw, 0, 80, nc.scalar)
         nc.vector.tensor_copy(v_picked[:], vs_win[:].indirect(cand_t[:]))
         place(v_plane, v_picked, 0)
         xs, es, vs = planes[:, 0:S], planes[:, S : 2 * S], v_plane[:]
-        cast_w(g1, w1_raw, 96, 128, nc.vector)
+        cast_w(g1, w1_raw, 80, 128, nc.vector)
         w1c, w1s = quantise(g1, H, "w1")
         cast_w(g2, w2_raw, 0, 64, nc.scalar)
         cast_w(g2, w2_raw, 64, 128, nc.vector)
@@ -131,26 +131,35 @@ def tile_picked_zfrs_relu_p_kernel(tc, x_words, x_scales, e_words, e_scales, w1,
         eg = [eg0[:], eg1[:], eg2[:, 0:CH], eg2[:, CH:]]
 
         yp = [psum.tile([P, V], F32, name=f"yp{c}") for c in range(n_ch)]
-        for c in range(3):
+        for c in range(2):
             nc.tensor.matmul_mx(out=yp[c][:], lhsT=w1c[:, 0:P].bitcast(FP8X4), lhsT_scale=w1s[:, 0:P],
                                 rhs=w1c[:].bitcast(FP8X4), rhs_scale=w1s[:], start=True, stop=True)
-        hb = []
-        for c in range(n_ch):
-            cols = slice(c * CH, (c + 1) * CH)
-            if c == 2:
-                xg_b = keep.tile([P, 2 * CH], U32, name="xg_b", tag="eg0", align_bytes=64)
-                for b in range(2):
-                    nc.vector.tensor_copy(xg_b[:, b * CH : (b + 1) * CH], x_win[:].bitcast(U32).indirect(offs_t[:, (2 + b) * CH // 16 : (3 + b) * CH // 16]))
-                xg.extend([xg_b[:, 0:CH], xg_b[:, CH:]])
-            hp = psum.tile([P, PACK, CH], F32, name=f"hp{c}")
+        hp = [psum.tile([P, PACK, CH], F32, name=f"hp{c}") for c in range(n_ch)]
+        hb = [tile([P, CH * PACK], BF16, f"hb{c}") for c in range(n_ch)]
+
+        def passes(c, codes, scales, words, plane, first):
             for t in range(PACK):
                 wc = slice(t * P, (t + 1) * P)
-                nc.tensor.matmul_mx(out=hp[:, t, :], lhsT=w1c[:, wc].bitcast(FP8X4), lhsT_scale=w1s[:, wc],
-                                    rhs=xg[c].bitcast(FP8X4), rhs_scale=xs[:, cols], start=True, stop=False)
-                nc.tensor.matmul_mx(out=hp[:, t, :], lhsT=w2c[:, wc].bitcast(FP8X4), lhsT_scale=w2s[:, wc],
-                                    rhs=eg[c].bitcast(FP8X4), rhs_scale=es[:, cols], start=False, stop=True)
-            hb.append(tile([P, CH * PACK], BF16, f"hb{c}"))
-            nc.scalar.activation(hb[c][:].rearrange("p (n t) -> p n t", t=PACK), hp[:].rearrange("p t n -> p n t"), ACT.Relu)
+                nc.tensor.matmul_mx(out=hp[c][:, t, :], lhsT=codes[:, wc].bitcast(FP8X4), lhsT_scale=scales[:, wc],
+                                    rhs=words.bitcast(FP8X4), rhs_scale=plane[:, c * CH : (c + 1) * CH],
+                                    start=first and t == 0, stop=not first and t == PACK - 1)
+
+        def relu(c):
+            nc.scalar.activation(hb[c][:].rearrange("p (n t) -> p n t", t=PACK), hp[c][:].rearrange("p t n -> p n t"), ACT.Relu)
+
+        for c in range(2):
+            passes(c, w1c, w1s, xg[c], xs, True)
+        for c in range(2):
+            passes(c, w2c, w2s, eg[c], es, False)
+            relu(c)
+        xg_b = keep.tile([P, 2 * CH], U32, name="xg_b", tag="eg0", align_bytes=64)
+        for c in range(2, n_ch):
+            passes(c, w2c, w2s, eg[c], es, True)
+        for c in range(2, n_ch):
+            words = xg_b[:, (c - 2) * CH : (c - 1) * CH]
+            nc.vector.tensor_copy(words, x_win[:].bitcast(U32).indirect(offs_t[:, c * CH // 16 : (c + 1) * CH // 16]))
+            passes(c, w1c, w1s, words, xs, False)
+            relu(c)
 
         HV = V // 2
         vg = [gather(v_win[:].bitcast(U32), cand_t[:, u * HV // 16 : (u + 1) * HV // 16], U32, f"vg{u}") for u in range(2)]

@@ -132,7 +132,7 @@ def tile_picked_zfrs_relu_p_kernel(tc, x_words, x_scales, e_words, e_scales, w1,
 
         yp = [psum.tile([P, V], F32, name=f"yp{c}") for c in range(n_ch)]
         for c in range(2):
-            nc.tensor.matmul_mx(out=yp[c][:], lhsT=w1c[:, 0:P].bitcast(FP8X4), lhsT_scale=w1s[:, 0:P],
+            nc.tensor.matmul_mx(out=yp[c][0:32, :], lhsT=w1c[:, 0:32].bitcast(FP8X4), lhsT_scale=w1s[:, 0:32],
                                 rhs=w1c[:].bitcast(FP8X4), rhs_scale=w1s[:], start=True, stop=True)
         hp = [psum.tile([P, PACK, CH], F32, name=f"hp{c}") for c in range(n_ch)]
         hb = [tile([P, CH * PACK], BF16, f"hb{c}") for c in range(n_ch)]

@@ -20,6 +20,7 @@ H = 512
 S = 512
 V = 512
 CH = 128
+LEAD = 512
 FLOPS = 2 * (2 * K * H * S + H * S * V)
 
 
@@ -80,21 +81,20 @@ def tile_picked_zfrs_relu_p_kernel(tc, x_words, x_scales, e_words, e_scales, w1,
         planes = tile([P, 2 * S], U8, "planes")
         v_plane = tile([P, V], U8, "v_plane")
         nc.vector.memset(planes[:].bitcast(I32), 0)
-        nc.vector.memset(v_plane[:].bitcast(I32), 0)
         warm = tile([P, 1], F32, "warm")
         warm_out = tile([P, 1], F32, "warm_out")
         nc.vector.memset(warm[:], 0.0)
 
         w1_raw = tile([P, PACK, H], F32, "w1_raw")
-        w1_rows = w1.rearrange("(p j) c -> p j c", j=PACK)
-        nc.sync.dma_start(w1_raw[:, 0:1, :], w1_rows[:, 0:1, :])
+        w1_rows = w1.rearrange("(p j) c -> p (j c)", j=PACK)
+        w1_flat = w1_raw[:].rearrange("p j c -> p (j c)")
+        nc.sync.dma_start(w1_flat[:, 0:LEAD], w1_rows[:, 0:LEAD])
         offs_t = load_list(offs, "offs_t")
         load_scales(xs_win, x_scales)
         nc.scalar.activation(warm_out[:], warm[:], ACT.Exp)
-        nc.sync.dma_start(w1_raw[:, 1:2, :], w1_rows[:, 1:2, :])
         tok_t = load_list(tok, "tok_t")
         load_scales(es_win, e_scales)
-        nc.sync.dma_start(w1_raw[:, 2:4, :], w1_rows[:, 2:4, :])
+        nc.sync.dma_start(w1_flat[:, LEAD:], w1_rows[:, LEAD:])
         cand_t = load_list(cand, "cand_t")
         load_scales(vs_win, v_scales)
         w2_raw = load_w(w2, "w2_raw")
@@ -115,10 +115,11 @@ def tile_picked_zfrs_relu_p_kernel(tc, x_words, x_scales, e_words, e_scales, w1,
         v_win = load_words(v_words, "v_win")
         cast_w(g1, w1_raw, 0, 80, nc.scalar)
         nc.vector.tensor_copy(v_picked[:], vs_win[:].indirect(cand_t[:]))
-        place(v_plane, v_picked, 0)
         xs, es, vs = planes[:, 0:S], planes[:, S : 2 * S], v_plane[:]
         cast_w(g1, w1_raw, 80, 128, nc.vector)
         w1c, w1s = quantise(g1, H, "w1")
+        nc.vector.tensor_copy(v_plane[:].bitcast(I32), v_picked[:].bitcast(I32))
+        place(v_plane, v_picked, 1)
         cast_w(g2, w2_raw, 0, 64, nc.scalar)
         cast_w(g2, w2_raw, 64, 128, nc.vector)
         xg_a = gather(x_win[:].bitcast(U32), offs_t[:, 0 : 2 * CH // 16], U32, "xg_a")
@@ -147,11 +148,12 @@ def tile_picked_zfrs_relu_p_kernel(tc, x_words, x_scales, e_words, e_scales, w1,
         def relu(c):
             nc.scalar.activation(hb[c][:].rearrange("p (n t) -> p n t", t=PACK), hp[c][:].rearrange("p t n -> p n t"), ACT.Relu)
 
-        for c in range(2):
-            passes(c, w1c, w1s, xg[c], xs, True)
-        for c in range(2):
-            passes(c, w2c, w2s, eg[c], es, False)
-            relu(c)
+        passes(0, w1c, w1s, xg[0], xs, True)
+        passes(0, w2c, w2s, eg[0], es, False)
+        relu(0)
+        passes(1, w2c, w2s, eg[1], es, True)
+        passes(1, w1c, w1s, xg[1], xs, False)
+        relu(1)
         xg_b = keep.tile([P, 2 * CH], U32, name="xg_b", tag="eg0", align_bytes=64)
         for c in range(2, n_ch):
             passes(c, w2c, w2s, eg[c], es, True)

@@ -43,8 +43,8 @@ def tile_picked_zfrs_relu_p_kernel(tc, x_words, x_scales, e_words, e_scales, w1,
             eng.memset(t[:].bitcast(I32), 0)
             return t
 
-        def load_scales(t, src):
-            nc.sync.dma_start(t[0:P:8, :].bitcast(I32), src[0].bitcast(I32))
+        def load_scales(t, src, first):
+            nc.sync.dma_start(t[first:P:8, :].bitcast(I32), src[0].bitcast(I32))
 
         def load_words(src, name):
             t = tile([P, src.shape[2]], I32, name)
@@ -90,19 +90,19 @@ def tile_picked_zfrs_relu_p_kernel(tc, x_words, x_scales, e_words, e_scales, w1,
         w1_flat = w1_raw[:].rearrange("p j c -> p (j c)")
         nc.sync.dma_start(w1_flat[:, 0:LEAD], w1_rows[:, 0:LEAD])
         offs_t = load_list(offs, "offs_t")
-        load_scales(xs_win, x_scales)
+        load_scales(xs_win, x_scales, 4)
         nc.scalar.activation(warm_out[:], warm[:], ACT.Exp)
         tok_t = load_list(tok, "tok_t")
-        load_scales(es_win, e_scales)
+        load_scales(es_win, e_scales, 4)
         nc.sync.dma_start(w1_flat[:, LEAD:], w1_rows[:, LEAD:])
         cand_t = load_list(cand, "cand_t")
-        load_scales(vs_win, v_scales)
+        load_scales(vs_win, v_scales, 0)
         w2_raw = load_w(w2, "w2_raw")
         x_win = load_words(x_words, "x_win")
 
-        def place(dst, src, first):
+        def place(dst, src, first, shift):
             for r in range(first, 4):
-                nc.sync.dma_start(dst[r:P:32, :].bitcast(I32), src[8 * r : P : 32, :].bitcast(I32))
+                nc.sync.dma_start(dst[r:P:32, :].bitcast(I32), src[shift + 8 * r : P : 32, :].bitcast(I32))
 
         g1 = tile([P, PACK * H], BF16, "g1")
         g2 = tile([P, PACK * H], BF16, "g2")
@@ -110,7 +110,7 @@ def tile_picked_zfrs_relu_p_kernel(tc, x_words, x_scales, e_words, e_scales, w1,
         v_picked = tile([P, V], U8, "v_picked")
         nc.vector.tensor_copy(picked[:, 0:S], xs_win[:].indirect(offs_t[:]))
         nc.vector.tensor_copy(picked[:, S : 2 * S], es_win[:].indirect(tok_t[:]))
-        place(planes, picked, 0)
+        place(planes, picked, 0, 4)
         e_win = load_words(e_words, "e_win")
         v_win = load_words(v_words, "v_win")
         cast_w(g1, w1_raw, 0, 80, nc.scalar)
@@ -119,7 +119,7 @@ def tile_picked_zfrs_relu_p_kernel(tc, x_words, x_scales, e_words, e_scales, w1,
         cast_w(g1, w1_raw, 80, 128, nc.vector)
         w1c, w1s = quantise(g1, H, "w1")
         nc.vector.tensor_copy(v_plane[:].bitcast(I32), v_picked[:].bitcast(I32))
-        place(v_plane, v_picked, 1)
+        place(v_plane, v_picked, 1, 0)
         cast_w(g2, w2_raw, 0, 64, nc.scalar)
         cast_w(g2, w2_raw, 64, 128, nc.vector)
         xg_a = gather(x_win[:].bitcast(U32), offs_t[:, 0 : 2 * CH // 16], U32, "xg_a")

@@ -21,6 +21,9 @@ S = 512
 V = 512
 CH = 128
 LEAD = 512
+FIRST = 256
+S1 = 80
+S2 = 64
 FLOPS = 2 * (2 * K * H * S + H * S * V)
 
 
@@ -77,7 +80,9 @@ def tile_picked_zfrs_relu_p_kernel(tc, x_words, x_scales, e_words, e_scales, w1,
 
         xs_win = clear_scales(x_scales, "xs_win", nc.vector)
         es_win = clear_scales(e_scales, "es_win", nc.vector)
-        vs_win = clear_scales(v_scales, "vs_win", nc.vector)
+        vs_win = tile([P, v_scales.shape[2]], U8, "vs_win")
+        for lo in range(0, v_scales.shape[2], 1024):
+            nc.vector.memset(vs_win[:, lo : lo + 1024].bitcast(I32), 0)
         planes = tile([P, 2 * S], U8, "planes")
         v_plane = tile([P, V], U8, "v_plane")
         nc.vector.memset(planes[:].bitcast(I32), 0)
@@ -113,15 +118,15 @@ def tile_picked_zfrs_relu_p_kernel(tc, x_words, x_scales, e_words, e_scales, w1,
         place(planes, picked, 0, 4)
         e_win = load_words(e_words, "e_win")
         v_win = load_words(v_words, "v_win")
-        cast_w(g1, w1_raw, 0, 80, nc.scalar)
+        cast_w(g1, w1_raw, 0, S1, nc.scalar)
         nc.vector.tensor_copy(v_picked[:], vs_win[:].indirect(cand_t[:]))
         xs, es, vs = planes[:, 0:S], planes[:, S : 2 * S], v_plane[:]
-        cast_w(g1, w1_raw, 80, 128, nc.vector)
+        cast_w(g1, w1_raw, S1, 128, nc.vector)
         w1c, w1s = quantise(g1, H, "w1")
         nc.vector.tensor_copy(v_plane[:].bitcast(I32), v_picked[:].bitcast(I32))
         place(v_plane, v_picked, 1, 0)
-        cast_w(g2, w2_raw, 0, 64, nc.scalar)
-        cast_w(g2, w2_raw, 64, 128, nc.vector)
+        cast_w(g2, w2_raw, 0, S2, nc.scalar)
+        cast_w(g2, w2_raw, S2, 128, nc.vector)
         xg_a = gather(x_win[:].bitcast(U32), offs_t[:, 0 : 2 * CH // 16], U32, "xg_a")
         w2c, w2s = quantise(g2, H, "w2")
         n_ch = S // CH
@@ -157,7 +162,6 @@ def tile_picked_zfrs_relu_p_kernel(tc, x_words, x_scales, e_words, e_scales, w1,
         xg_b = keep.tile([P, 2 * CH], U32, name="xg_b", tag="eg0", align_bytes=64)
         for c in range(2, n_ch):
             passes(c, w2c, w2s, eg[c], es, True)
-        for c in range(2, n_ch):
             words = xg_b[:, (c - 2) * CH : (c - 1) * CH]
             nc.vector.tensor_copy(words, x_win[:].bitcast(U32).indirect(offs_t[:, c * CH // 16 : (c + 1) * CH // 16]))
             passes(c, w1c, w1s, words, xs, False)
@@ -171,16 +175,16 @@ def tile_picked_zfrs_relu_p_kernel(tc, x_words, x_scales, e_words, e_scales, w1,
 
         def quantise_h(c):
             cols = slice(c * CH, (c + 1) * CH)
-            h_scales = keep.tile([P, CH], U8, name=f"h_scales{c}", tag=f"h_scales{c % 3}", align_bytes=64)
+            h_scales = keep.tile([P, CH], U8, name=f"h_scales{c}", tag=f"h_scales{c}", align_bytes=64)
             codes = h_first[:] if c == 0 else h_codes[:, cols]
             nc.vector.quantize_mx(out=codes.bitcast(FP8X4), scales=h_scales[:], in_=hb[c][:])
             hq.append((codes, h_scales[:]))
 
-        for c in range(3):
+        for c in range(n_ch):
             quantise_h(c)
 
         ex = [tile([P, V], F32, f"ex{c}") for c in range(n_ch)]
-        total = [tile([P, 1], F32, f"total{c}") for c in range(n_ch)]
+        total = [keep.tile([P, 1], F32, name=f"total{c}", tag=f"total{c % 2 if c < 3 else c}", align_bytes=64) for c in range(n_ch)]
         inv = [tile([P, 1], F32, f"inv{c}") for c in range(n_ch)]
 
         def logits(c):
@@ -189,7 +193,7 @@ def tile_picked_zfrs_relu_p_kernel(tc, x_words, x_scales, e_words, e_scales, w1,
                 vc = slice(u * HV, (u + 1) * HV)
                 nc.tensor.matmul_mx(out=yp[c][:, vc], lhsT=hc.bitcast(FP8X4), lhsT_scale=hs,
                                     rhs=vg[u][:].bitcast(FP8X4), rhs_scale=vs[:, vc], start=True, stop=True)
-            negmax = tile([P, 1], F32, f"negmax{c}")
+            negmax = keep.tile([P, 1], F32, name=f"negmax{c}", tag=f"negmax{c % 3}", align_bytes=64)
             nc.vector.tensor_reduce(negmax[:], yp[c][:], AX.X, ALU.max, negate=True)
             nc.scalar.activation(ex[c][:], yp[c][:], ACT.Exp, bias=negmax[:], scale=1.0, accum_out=total[c][:])
 
@@ -202,16 +206,16 @@ def tile_picked_zfrs_relu_p_kernel(tc, x_words, x_scales, e_words, e_scales, w1,
             nc.sync.dma_start(out[c * CH : (c + 1) * CH, :], res[:])
 
         logits(0)
-        quantise_h(3)
         logits(1)
-        logits(2)
         invert(0)
+        res_first = tile([P, V], F32, "res_first")
+        nc.scalar.activation(res_first[:, 0:FIRST], ex[0][:, 0:FIRST], ACT.Copy, scale=inv[0][:])
+        nc.sync.dma_start(out[0:CH, 0:FIRST], res_first[:, 0:FIRST])
+        logits(2)
         logits(3)
+        nc.vector.tensor_scalar(res_first[:, FIRST:], ex[0][:, FIRST:], inv[0][:], None, ALU.mult)
+        nc.sync.dma_start(out[0:CH, FIRST:], res_first[:, FIRST:])
         invert(1)
-        for u in range(2):
-            half = tile([P, HV], F32, f"res_first{u}")
-            nc.vector.tensor_scalar(half[:], ex[0][:, u * HV : (u + 1) * HV], inv[0][:], None, ALU.mult)
-            nc.sync.dma_start(out[0:CH, u * HV : (u + 1) * HV], half[:])
         invert(2)
         finish(1)
         finish(2)

@@ -20,10 +20,11 @@ H = 512
 S = 512
 V = 512
 CH = 128
+TOP = P - 16
 LEAD = 512
 FIRST = 256
-S1 = 80
-S2 = 64
+S1 = 72
+S2 = 72
 FLOPS = 2 * (2 * K * H * S + H * S * V)
 
 
@@ -78,8 +79,10 @@ def tile_picked_zfrs_relu_p_kernel(tc, x_words, x_scales, e_words, e_scales, w1,
             nc.vector.tensor_copy(t[:], window.indirect(offsets))
             return t
 
-        xs_win = clear_scales(x_scales, "xs_win", nc.vector)
-        es_win = clear_scales(e_scales, "es_win", nc.vector)
+        xs_win = tile([P, x_scales.shape[2]], U8, "xs_win")
+        es_win = tile([P, e_scales.shape[2]], U8, "es_win")
+        nc.vector.memset(xs_win[0:TOP, :].bitcast(I32), 0)
+        nc.vector.memset(es_win[0:TOP, :].bitcast(I32), 0)
         vs_win = tile([P, v_scales.shape[2]], U8, "vs_win")
         for lo in range(0, v_scales.shape[2], 1024):
             nc.vector.memset(vs_win[:, lo : lo + 1024].bitcast(I32), 0)
@@ -93,15 +96,15 @@ def tile_picked_zfrs_relu_p_kernel(tc, x_words, x_scales, e_words, e_scales, w1,
         w1_raw = tile([P, PACK, H], F32, "w1_raw")
         w1_rows = w1.rearrange("(p j) c -> p (j c)", j=PACK)
         w1_flat = w1_raw[:].rearrange("p j c -> p (j c)")
-        nc.sync.dma_start(w1_flat[:, 0:LEAD], w1_rows[:, 0:LEAD])
         offs_t = load_list(offs, "offs_t")
-        load_scales(xs_win, x_scales, 4)
-        nc.scalar.activation(warm_out[:], warm[:], ACT.Exp)
+        nc.sync.dma_start(w1_flat[:, 0:LEAD], w1_rows[:, 0:LEAD])
+        nc.scalar.dma_start(xs_win[TOP:P, :].bitcast(I32), x_scales[0].bitcast(I32))
         tok_t = load_list(tok, "tok_t")
-        load_scales(es_win, e_scales, 4)
+        nc.scalar.dma_start(es_win[TOP:P, :].bitcast(I32), e_scales[0].bitcast(I32))
         nc.sync.dma_start(w1_flat[:, LEAD:], w1_rows[:, LEAD:])
         cand_t = load_list(cand, "cand_t")
         load_scales(vs_win, v_scales, 0)
+        nc.scalar.activation(warm_out[:], warm[:], ACT.Exp)
         w2_raw = load_w(w2, "w2_raw")
         x_win = load_words(x_words, "x_win")
 
@@ -115,7 +118,8 @@ def tile_picked_zfrs_relu_p_kernel(tc, x_words, x_scales, e_words, e_scales, w1,
         v_picked = tile([P, V], U8, "v_picked")
         nc.vector.tensor_copy(picked[:, 0:S], xs_win[:].indirect(offs_t[:]))
         nc.vector.tensor_copy(picked[:, S : 2 * S], es_win[:].indirect(tok_t[:]))
-        place(planes, picked, 0, 4)
+        for r in range(4):
+            nc.sync.dma_start(planes[r:P:32, :].bitcast(I32), picked[TOP + r : P : 4, :].bitcast(I32))
         e_win = load_words(e_words, "e_win")
         v_win = load_words(v_words, "v_win")
         cast_w(g1, w1_raw, 0, S1, nc.scalar)
@@ -137,7 +141,7 @@ def tile_picked_zfrs_relu_p_kernel(tc, x_words, x_scales, e_words, e_scales, w1,
         eg = [eg0[:], eg1[:], eg2[:, 0:CH], eg2[:, CH:]]
 
         yp = [psum.tile([P, V], F32, name=f"yp{c}") for c in range(n_ch)]
-        for c in range(2):
+        for c in range(3):
             nc.tensor.matmul_mx(out=yp[c][0:32, :], lhsT=w1c[:, 0:32].bitcast(FP8X4), lhsT_scale=w1s[:, 0:32],
                                 rhs=w1c[:].bitcast(FP8X4), rhs_scale=w1s[:], start=True, stop=True)
         hp = [psum.tile([P, PACK, CH], F32, name=f"hp{c}") for c in range(n_ch)]

@@ -35,7 +35,7 @@ def tile_picked_zfrs_relu_p_kernel(tc, x_words, x_scales, e_words, e_scales, w1,
         psum = ctx.enter_context(tc.psum_pool(name="psum", bufs=1))
 
         def tile(shape, dtype, name):
-            return keep.tile(shape, dtype, name=name, align_bytes=64)
+            return keep.tile(shape, dtype, name=name, align_bytes=256)
 
         def load_list(src, name):
             t = keep.tile([P, src.shape[1]], U16, name=name)
@@ -163,7 +163,7 @@ def tile_picked_zfrs_relu_p_kernel(tc, x_words, x_scales, e_words, e_scales, w1,
         passes(1, w2c, w2s, eg[1], es, True)
         passes(1, w1c, w1s, xg[1], xs, False)
         relu(1)
-        xg_b = keep.tile([P, 2 * CH], U32, name="xg_b", tag="eg0", align_bytes=64)
+        xg_b = keep.tile([P, 2 * CH], U32, name="xg_b", tag="eg0", align_bytes=256)
         for c in range(2, n_ch):
             passes(c, w2c, w2s, eg[c], es, True)
             words = xg_b[:, (c - 2) * CH : (c - 1) * CH]
@@ -173,7 +173,7 @@ def tile_picked_zfrs_relu_p_kernel(tc, x_words, x_scales, e_words, e_scales, w1,
 
         HV = V // 2
         vg = [gather(v_win[:].bitcast(U32), cand_t[:, u * HV // 16 : (u + 1) * HV // 16], U32, f"vg{u}") for u in range(2)]
-        h_codes = keep.tile([P, S], U32, name="h_codes", tag="v_win", align_bytes=64)
+        h_codes = keep.tile([P, S], U32, name="h_codes", tag="v_win", align_bytes=256)
         h_first = tile([P, CH], U32, "h_first")
         hq = []
 

@@ -21,6 +21,8 @@ S = 512
 V = 512
 CH = 128
 TOP = P - 16
+V_ROW = 40
+V_PLANE = 12
 LEAD = 512
 FIRST = 256
 S1 = 72
@@ -48,7 +50,7 @@ def tile_picked_zfrs_relu_p_kernel(tc, x_words, x_scales, e_words, e_scales, w1,
             return t
 
         def load_scales(t, src, first):
-            nc.sync.dma_start(t[first:P:8, :].bitcast(I32), src[0].bitcast(I32))
+            nc.sync.dma_start(t[first : first + 16, :].bitcast(I32), src[0].bitcast(I32))
 
         def load_words(src, name):
             t = tile([P, src.shape[2]], I32, name)
@@ -96,21 +98,21 @@ def tile_picked_zfrs_relu_p_kernel(tc, x_words, x_scales, e_words, e_scales, w1,
         w1_raw = tile([P, PACK, H], F32, "w1_raw")
         w1_rows = w1.rearrange("(p j) c -> p (j c)", j=PACK)
         w1_flat = w1_raw[:].rearrange("p j c -> p (j c)")
-        offs_t = load_list(offs, "offs_t")
         nc.sync.dma_start(w1_flat[:, 0:LEAD], w1_rows[:, 0:LEAD])
+        offs_t = load_list(offs, "offs_t")
         nc.scalar.dma_start(xs_win[TOP:P, :].bitcast(I32), x_scales[0].bitcast(I32))
         tok_t = load_list(tok, "tok_t")
         nc.scalar.dma_start(es_win[TOP:P, :].bitcast(I32), e_scales[0].bitcast(I32))
         nc.sync.dma_start(w1_flat[:, LEAD:], w1_rows[:, LEAD:])
         cand_t = load_list(cand, "cand_t")
-        load_scales(vs_win, v_scales, 0)
+        load_scales(vs_win, v_scales, V_ROW)
         nc.scalar.activation(warm_out[:], warm[:], ACT.Exp)
         w2_raw = load_w(w2, "w2_raw")
         x_win = load_words(x_words, "x_win")
 
-        def place(dst, src, first, shift):
-            for r in range(first, 4):
-                nc.sync.dma_start(dst[r:P:32, :].bitcast(I32), src[shift + 8 * r : P : 32, :].bitcast(I32))
+        def place_v(q):
+            to, at = 32 * q + V_PLANE, V_ROW + 4 * q
+            nc.sync.dma_start(v_plane[to : to + 4, :].bitcast(I32), v_picked[at : at + 4, :].bitcast(I32))
 
         g1 = tile([P, PACK * H], BF16, "g1")
         g2 = tile([P, PACK * H], BF16, "g2")
@@ -124,11 +126,12 @@ def tile_picked_zfrs_relu_p_kernel(tc, x_words, x_scales, e_words, e_scales, w1,
         v_win = load_words(v_words, "v_win")
         cast_w(g1, w1_raw, 0, S1, nc.scalar)
         nc.vector.tensor_copy(v_picked[:], vs_win[:].indirect(cand_t[:]))
-        xs, es, vs = planes[:, 0:S], planes[:, S : 2 * S], v_plane[:]
+        xs, es, vs = planes[:, 0:S], planes[:, S : 2 * S], v_plane[V_PLANE:P, :]
         cast_w(g1, w1_raw, S1, 128, nc.vector)
         w1c, w1s = quantise(g1, H, "w1")
         nc.vector.tensor_copy(v_plane[:].bitcast(I32), v_picked[:].bitcast(I32))
-        place(v_plane, v_picked, 1, 0)
+        for q in (0, 2, 3):
+            place_v(q)
         cast_w(g2, w2_raw, 0, S2, nc.scalar)
         cast_w(g2, w2_raw, S2, 128, nc.vector)
         xg_a = gather(x_win[:].bitcast(U32), offs_t[:, 0 : 2 * CH // 16], U32, "xg_a")

@@ -34,6 +34,7 @@ def tile_picked_zfrs_relu_p_kernel(tc, x_words, x_scales, e_words, e_scales, w1,
     nc = tc.nc
     with ExitStack() as ctx:
         keep = ctx.enter_context(tc.tile_pool(name="keep", bufs=1))
+        late = ctx.enter_context(tc.tile_pool(name="late", bufs=1))
         psum = ctx.enter_context(tc.psum_pool(name="psum", bufs=1))
 
         def tile(shape, dtype, name):
@@ -81,25 +82,24 @@ def tile_picked_zfrs_relu_p_kernel(tc, x_words, x_scales, e_words, e_scales, w1,
             nc.vector.tensor_copy(t[:], window.indirect(offsets))
             return t
 
-        xs_win = tile([P, x_scales.shape[2]], U8, "xs_win")
-        es_win = tile([P, e_scales.shape[2]], U8, "es_win")
-        nc.vector.memset(xs_win[0:TOP, :].bitcast(I32), 0)
-        nc.vector.memset(es_win[0:TOP, :].bitcast(I32), 0)
-        vs_win = tile([P, v_scales.shape[2]], U8, "vs_win")
-        for lo in range(0, v_scales.shape[2], 1024):
-            nc.vector.memset(vs_win[:, lo : lo + 1024].bitcast(I32), 0)
-        planes = tile([P, 2 * S], U8, "planes")
-        v_plane = tile([P, V], U8, "v_plane")
-        nc.vector.memset(planes[:].bitcast(I32), 0)
         warm = tile([P, 1], F32, "warm")
         warm_out = tile([P, 1], F32, "warm_out")
-        nc.vector.memset(warm[:], 0.0)
+        nc.gpsimd.memset(warm[:], 0.0)
+        xs_win = tile([P, x_scales.shape[2]], U8, "xs_win")
+        es_win = tile([P, e_scales.shape[2]], U8, "es_win")
+        nc.gpsimd.memset(xs_win[0:TOP, :].bitcast(I32), 0)
+        nc.gpsimd.memset(es_win[0:TOP, :].bitcast(I32), 0)
+        vs_win = tile([P, v_scales.shape[2]], U8, "vs_win")
+        nc.gpsimd.memset(vs_win[:].bitcast(I32), 0)
+        planes = tile([P, 2 * S], U8, "planes")
+        v_plane = tile([P, V], U8, "v_plane")
+        nc.gpsimd.memset(planes[:].bitcast(I32), 0)
 
         w1_raw = tile([P, PACK, H], F32, "w1_raw")
         w1_rows = w1.rearrange("(p j) c -> p (j c)", j=PACK)
         w1_flat = w1_raw[:].rearrange("p j c -> p (j c)")
-        nc.sync.dma_start(w1_flat[:, 0:LEAD], w1_rows[:, 0:LEAD])
         offs_t = load_list(offs, "offs_t")
+        nc.sync.dma_start(w1_flat[:, 0:LEAD], w1_rows[:, 0:LEAD])
         nc.scalar.dma_start(xs_win[TOP:P, :].bitcast(I32), x_scales[0].bitcast(I32))
         tok_t = load_list(tok, "tok_t")
         nc.scalar.dma_start(es_win[TOP:P, :].bitcast(I32), e_scales[0].bitcast(I32))
@@ -117,7 +117,7 @@ def tile_picked_zfrs_relu_p_kernel(tc, x_words, x_scales, e_words, e_scales, w1,
         g1 = tile([P, PACK * H], BF16, "g1")
         g2 = tile([P, PACK * H], BF16, "g2")
         picked = tile([P, 2 * S], U8, "picked")
-        v_picked = tile([P, V], U8, "v_picked")
+        v_picked = late.tile([P, 4 * V], U8, name="v_picked", offset=0, align_bytes=256)[:, 0:V]
         nc.vector.tensor_copy(picked[:, 0:S], xs_win[:].indirect(offs_t[:]))
         nc.vector.tensor_copy(picked[:, S : 2 * S], es_win[:].indirect(tok_t[:]))
         for r in range(4):
@@ -125,11 +125,11 @@ def tile_picked_zfrs_relu_p_kernel(tc, x_words, x_scales, e_words, e_scales, w1,
         e_win = load_words(e_words, "e_win")
         v_win = load_words(v_words, "v_win")
         cast_w(g1, w1_raw, 0, S1, nc.scalar)
-        nc.vector.tensor_copy(v_picked[:], vs_win[:].indirect(cand_t[:]))
+        nc.vector.tensor_copy(v_picked, vs_win[:].indirect(cand_t[:]))
         xs, es, vs = planes[:, 0:S], planes[:, S : 2 * S], v_plane[V_PLANE:P, :]
         cast_w(g1, w1_raw, S1, 128, nc.vector)
         w1c, w1s = quantise(g1, H, "w1")
-        nc.vector.tensor_copy(v_plane[:].bitcast(I32), v_picked[:].bitcast(I32))
+        nc.vector.tensor_copy(v_plane[:].bitcast(I32), v_picked.bitcast(I32))
         for q in (0, 2, 3):
             place_v(q)
         cast_w(g2, w2_raw, 0, S2, nc.scalar)
@@ -167,28 +167,28 @@ def tile_picked_zfrs_relu_p_kernel(tc, x_words, x_scales, e_words, e_scales, w1,
         passes(1, w1c, w1s, xg[1], xs, False)
         relu(1)
         xg_b = keep.tile([P, 2 * CH], U32, name="xg_b", tag="eg0", align_bytes=256)
+        nc.vector.tensor_copy(xg_b[:], x_win[:].bitcast(U32).indirect(offs_t[:, 2 * CH // 16 :]))
         for c in range(2, n_ch):
             passes(c, w2c, w2s, eg[c], es, True)
-            words = xg_b[:, (c - 2) * CH : (c - 1) * CH]
-            nc.vector.tensor_copy(words, x_win[:].bitcast(U32).indirect(offs_t[:, c * CH // 16 : (c + 1) * CH // 16]))
-            passes(c, w1c, w1s, words, xs, False)
+            passes(c, w1c, w1s, xg_b[:, (c - 2) * CH : (c - 1) * CH], xs, False)
             relu(c)
 
-        HV = V // 2
-        vg = [gather(v_win[:].bitcast(U32), cand_t[:, u * HV // 16 : (u + 1) * HV // 16], U32, f"vg{u}") for u in range(2)]
-        h_codes = keep.tile([P, S], U32, name="h_codes", tag="v_win", align_bytes=256)
-        h_first = tile([P, CH], U32, "h_first")
+        HV = V - CH
+        h_codes = [late.tile([P, CH], U32, name=f"h_codes{c}", offset=(c % 3) * V, align_bytes=256) for c in range(n_ch)]
         hq = []
 
         def quantise_h(c):
-            cols = slice(c * CH, (c + 1) * CH)
             h_scales = keep.tile([P, CH], U8, name=f"h_scales{c}", tag=f"h_scales{c}", align_bytes=64)
-            codes = h_first[:] if c == 0 else h_codes[:, cols]
+            codes = h_codes[c][:]
             nc.vector.quantize_mx(out=codes.bitcast(FP8X4), scales=h_scales[:], in_=hb[c][:])
             hq.append((codes, h_scales[:]))
 
-        for c in range(n_ch):
-            quantise_h(c)
+        vg = [gather(v_win[:].bitcast(U32), cand_t[:, 0 : HV // 16], U32, "vg0")]
+        quantise_h(0)
+        vg.append(late.tile([P, V - HV], U32, name="vg1", offset=3 * V, align_bytes=256))
+        nc.vector.tensor_copy(vg[1][:], v_win[:].bitcast(U32).indirect(cand_t[:, HV // 16 :]))
+        quantise_h(1)
+        quantise_h(2)
 
         ex = [tile([P, V], F32, f"ex{c}") for c in range(n_ch)]
         total = [keep.tile([P, 1], F32, name=f"total{c}", tag=f"total{c % 2 if c < 3 else c}", align_bytes=64) for c in range(n_ch)]
@@ -196,10 +196,9 @@ def tile_picked_zfrs_relu_p_kernel(tc, x_words, x_scales, e_words, e_scales, w1,
 
         def logits(c):
             hc, hs = hq[c]
-            for u in range(2):
-                vc = slice(u * HV, (u + 1) * HV)
-                nc.tensor.matmul_mx(out=yp[c][:, vc], lhsT=hc.bitcast(FP8X4), lhsT_scale=hs,
-                                    rhs=vg[u][:].bitcast(FP8X4), rhs_scale=vs[:, vc], start=True, stop=True)
+            for words, lo, hi in ((vg[0][:, 0:256], 0, 256), (vg[0][:, 256:], 256, HV), (vg[1][:], HV, V)):
+                nc.tensor.matmul_mx(out=yp[c][:, lo:hi], lhsT=hc.bitcast(FP8X4), lhsT_scale=hs,
+                                    rhs=words.bitcast(FP8X4), rhs_scale=vs[:, lo:hi], start=True, stop=True)
             negmax = keep.tile([P, 1], F32, name=f"negmax{c}", tag=f"negmax{c % 3}", align_bytes=64)
             nc.vector.tensor_reduce(negmax[:], yp[c][:], AX.X, ALU.max, negate=True)
             nc.scalar.activation(ex[c][:], yp[c][:], ACT.Exp, bias=negmax[:], scale=1.0, accum_out=total[c][:])
@@ -213,6 +212,7 @@ def tile_picked_zfrs_relu_p_kernel(tc, x_words, x_scales, e_words, e_scales, w1,
             nc.sync.dma_start(out[c * CH : (c + 1) * CH, :], res[:])
 
         logits(0)
+        quantise_h(3)
         logits(1)
         invert(0)
         res_first = tile([P, V], F32, "res_first")

@@ -25,8 +25,8 @@ V_ROW = 40
 V_PLANE = 12
 LEAD = 512
 FIRST = 256
-S1 = 72
-S2 = 72
+S1 = 104
+S2 = 84
 FLOPS = 2 * (2 * K * H * S + H * S * V)
 
 
@@ -98,8 +98,8 @@ def tile_picked_zfrs_relu_p_kernel(tc, x_words, x_scales, e_words, e_scales, w1,
         w1_raw = tile([P, PACK, H], F32, "w1_raw")
         w1_rows = w1.rearrange("(p j) c -> p (j c)", j=PACK)
         w1_flat = w1_raw[:].rearrange("p j c -> p (j c)")
-        offs_t = load_list(offs, "offs_t")
         nc.sync.dma_start(w1_flat[:, 0:LEAD], w1_rows[:, 0:LEAD])
+        offs_t = load_list(offs, "offs_t")
         nc.scalar.dma_start(xs_win[TOP:P, :].bitcast(I32), x_scales[0].bitcast(I32))
         tok_t = load_list(tok, "tok_t")
         nc.scalar.dma_start(es_win[TOP:P, :].bitcast(I32), e_scales[0].bitcast(I32))
@@ -128,8 +128,8 @@ def tile_picked_zfrs_relu_p_kernel(tc, x_words, x_scales, e_words, e_scales, w1,
         nc.vector.tensor_copy(v_picked, vs_win[:].indirect(cand_t[:]))
         xs, es, vs = planes[:, 0:S], planes[:, S : 2 * S], v_plane[V_PLANE:P, :]
         cast_w(g1, w1_raw, S1, 128, nc.vector)
-        w1c, w1s = quantise(g1, H, "w1")
         nc.vector.tensor_copy(v_plane[:].bitcast(I32), v_picked.bitcast(I32))
+        w1c, w1s = quantise(g1, H, "w1")
         for q in (0, 2, 3):
             place_v(q)
         cast_w(g2, w2_raw, 0, S2, nc.scalar)

from contextlib import ExitStack

import concourse.mybir as mybir

F32 = mybir.dt.float32
BF16 = mybir.dt.bfloat16
I32 = mybir.dt.int32
U32 = mybir.dt.uint32
U16 = mybir.dt.uint16
U8 = mybir.dt.uint8
FP8X4 = mybir.dt.float8_e4m3fn_x4
ACT = mybir.ActivationFunctionType
ALU = mybir.AluOpType
AX = mybir.AxisListType

P = 128
PACK = 4
K = 512
H = 512
S = 512
V = 512
CH = 128
TOP = P - 16
V_ROW = 40
V_PLANE = 12
LEAD = 512
FIRST = 256
S1 = 104
S2 = 84
FLOPS = 2 * (2 * K * H * S + H * S * V)


def tile_picked_zfrs_relu_p_kernel(tc, x_words, x_scales, e_words, e_scales, w1, w2, v_words, v_scales, offs, tok, cand, out):
    nc = tc.nc
    with ExitStack() as ctx:
        keep = ctx.enter_context(tc.tile_pool(name="keep", bufs=1))
        late = ctx.enter_context(tc.tile_pool(name="late", bufs=1))
        psum = ctx.enter_context(tc.psum_pool(name="psum", bufs=1))

        def tile(shape, dtype, name):
            return keep.tile(shape, dtype, name=name, align_bytes=256)

        def load_list(src, name):
            t = keep.tile([P, src.shape[1]], U16, name=name)
            nc.sync.dma_start(t[:], src)
            return t

        def clear_scales(src, name, eng):
            t = tile([P, src.shape[2]], U8, name)
            eng.memset(t[:].bitcast(I32), 0)
            return t

        def load_scales(t, src, first):
            nc.sync.dma_start(t[first : first + 16, :].bitcast(I32), src[0].bitcast(I32))

        def load_words(src, name):
            t = tile([P, src.shape[2]], I32, name)
            nc.sync.dma_start(t[:], src[0].rearrange("p n t -> p (n t)").bitcast(I32))
            return t

        def load_w(src, name):
            t = tile([P, PACK, H], F32, name)
            nc.sync.dma_start(t[:], src.rearrange("(p j) c -> p j c", j=PACK))
            return t

        def cast_w(grouped, raw, lo, hi, eng):
            dst = grouped[:].rearrange("p (t m j) -> p m j t", t=PACK, j=PACK)[:, lo:hi]
            src = raw[:].rearrange("p j (m t) -> p m j t", t=PACK)[:, lo:hi]
            if eng is nc.scalar:
                nc.scalar.copy(dst, src)
            else:
                nc.vector.tensor_copy(dst, src)

        def quantise(grouped, width, name):
            codes = tile([P, width], U32, name + "_codes")
            scales = tile([P, width], U8, name + "_scales")
            nc.vector.quantize_mx(out=codes[:].bitcast(FP8X4), scales=scales[:], in_=grouped[:])
            return codes, scales

        def gather(window, offsets, dtype, name):
            t = tile([P, 16 * offsets.shape[1]], dtype, name)
            nc.vector.tensor_copy(t[:], window.indirect(offsets))
            return t

        warm = tile([P, 1], F32, "warm")
        warm_out = tile([P, 1], F32, "warm_out")
        nc.gpsimd.memset(warm[:], 0.0)
        xs_win = tile([P, x_scales.shape[2]], U8, "xs_win")
        es_win = tile([P, e_scales.shape[2]], U8, "es_win")
        nc.gpsimd.memset(xs_win[0:TOP, :].bitcast(I32), 0)
        nc.gpsimd.memset(es_win[0:TOP, :].bitcast(I32), 0)
        vs_win = tile([P, v_scales.shape[2]], U8, "vs_win")
        nc.gpsimd.memset(vs_win[:].bitcast(I32), 0)
        planes = tile([P, 2 * S], U8, "planes")
        v_plane = tile([P, V], U8, "v_plane")
        nc.gpsimd.memset(planes[:].bitcast(I32), 0)

        w1_raw = tile([P, PACK, H], F32, "w1_raw")
        w1_rows = w1.rearrange("(p j) c -> p (j c)", j=PACK)
        w1_flat = w1_raw[:].rearrange("p j c -> p (j c)")
        nc.sync.dma_start(w1_flat[:, 0:LEAD], w1_rows[:, 0:LEAD])
        offs_t = load_list(offs, "offs_t")
        nc.scalar.dma_start(xs_win[TOP:P, :].bitcast(I32), x_scales[0].bitcast(I32))
        tok_t = load_list(tok, "tok_t")
        nc.scalar.dma_start(es_win[TOP:P, :].bitcast(I32), e_scales[0].bitcast(I32))
        nc.sync.dma_start(w1_flat[:, LEAD:], w1_rows[:, LEAD:])
        cand_t = load_list(cand, "cand_t")
        load_scales(vs_win, v_scales, V_ROW)
        nc.scalar.activation(warm_out[:], warm[:], ACT.Exp)
        w2_raw = load_w(w2, "w2_raw")
        x_win = load_words(x_words, "x_win")

        def place_v(q):
            to, at = 32 * q + V_PLANE, V_ROW + 4 * q
            nc.sync.dma_start(v_plane[to : to + 4, :].bitcast(I32), v_picked[at : at + 4, :].bitcast(I32))

        g1 = tile([P, PACK * H], BF16, "g1")
        g2 = tile([P, PACK * H], BF16, "g2")
        picked = tile([P, 2 * S], U8, "picked")
        v_picked = late.tile([P, 4 * V], U8, name="v_picked", offset=0, align_bytes=256)[:, 0:V]
        nc.vector.tensor_copy(picked[:, 0:S], xs_win[:].indirect(offs_t[:]))
        nc.vector.tensor_copy(picked[:, S : 2 * S], es_win[:].indirect(tok_t[:]))
        for r in range(4):
            nc.sync.dma_start(planes[r:P:32, :].bitcast(I32), picked[TOP + r : P : 4, :].bitcast(I32))
        e_win = load_words(e_words, "e_win")
        v_win = load_words(v_words, "v_win")
        cast_w(g1, w1_raw, 0, S1, nc.scalar)
        nc.vector.tensor_copy(v_picked, vs_win[:].indirect(cand_t[:]))
        xs, es, vs = planes[:, 0:S], planes[:, S : 2 * S], v_plane[V_PLANE:P, :]
        cast_w(g1, w1_raw, S1, 128, nc.vector)
        nc.vector.tensor_copy(v_plane[:].bitcast(I32), v_picked.bitcast(I32))
        w1c, w1s = quantise(g1, H, "w1")
        for q in (0, 2, 3):
            place_v(q)
        cast_w(g2, w2_raw, 0, S2, nc.scalar)
        cast_w(g2, w2_raw, S2, 128, nc.vector)
        xg_a = gather(x_win[:].bitcast(U32), offs_t[:, 0 : 2 * CH // 16], U32, "xg_a")
        w2c, w2s = quantise(g2, H, "w2")
        n_ch = S // CH
        eg0 = gather(e_win[:].bitcast(U32), tok_t[:, 0 : CH // 16], U32, "eg0")
        eg1 = gather(e_win[:].bitcast(U32), tok_t[:, CH // 16 : 2 * CH // 16], U32, "eg1")
        eg2 = gather(e_win[:].bitcast(U32), tok_t[:, 2 * CH // 16 :], U32, "eg2")
        xg = [xg_a[:, 0:CH], xg_a[:, CH:]]
        eg = [eg0[:], eg1[:], eg2[:, 0:CH], eg2[:, CH:]]

        yp = [psum.tile([P, V], F32, name=f"yp{c}") for c in range(n_ch)]
        for c in range(3):
            nc.tensor.matmul_mx(out=yp[c][0:32, :], lhsT=w1c[:, 0:32].bitcast(FP8X4), lhsT_scale=w1s[:, 0:32],
                                rhs=w1c[:].bitcast(FP8X4), rhs_scale=w1s[:], start=True, stop=True)
        hp = [psum.tile([P, PACK, CH], F32, name=f"hp{c}") for c in range(n_ch)]
        hb = [tile([P, CH * PACK], BF16, f"hb{c}") for c in range(n_ch)]

        def passes(c, codes, scales, words, plane, first):
            for t in range(PACK):
                wc = slice(t * P, (t + 1) * P)
                nc.tensor.matmul_mx(out=hp[c][:, t, :], lhsT=codes[:, wc].bitcast(FP8X4), lhsT_scale=scales[:, wc],
                                    rhs=words.bitcast(FP8X4), rhs_scale=plane[:, c * CH : (c + 1) * CH],
                                    start=first and t == 0, stop=not first and t == PACK - 1)

        def relu(c):
            nc.scalar.activation(hb[c][:].rearrange("p (n t) -> p n t", t=PACK), hp[c][:].rearrange("p t n -> p n t"), ACT.Relu)

        passes(0, w1c, w1s, xg[0], xs, True)
        passes(0, w2c, w2s, eg[0], es, False)
        relu(0)
        passes(1, w2c, w2s, eg[1], es, True)
        passes(1, w1c, w1s, xg[1], xs, False)
        relu(1)
        xg_b = keep.tile([P, 2 * CH], U32, name="xg_b", tag="eg0", align_bytes=256)
        nc.vector.tensor_copy(xg_b[:], x_win[:].bitcast(U32).indirect(offs_t[:, 2 * CH // 16 :]))
        for c in range(2, n_ch):
            passes(c, w2c, w2s, eg[c], es, True)
            passes(c, w1c, w1s, xg_b[:, (c - 2) * CH : (c - 1) * CH], xs, False)
            relu(c)

        HV = V - CH
        h_codes = [late.tile([P, CH], U32, name=f"h_codes{c}", offset=(c % 3) * V, align_bytes=256) for c in range(n_ch)]
        hq = []

        def quantise_h(c):
            h_scales = keep.tile([P, CH], U8, name=f"h_scales{c}", tag=f"h_scales{c}", align_bytes=64)
            codes = h_codes[c][:]
            nc.vector.quantize_mx(out=codes.bitcast(FP8X4), scales=h_scales[:], in_=hb[c][:])
            hq.append((codes, h_scales[:]))

        vg = [gather(v_win[:].bitcast(U32), cand_t[:, 0 : HV // 16], U32, "vg0")]
        quantise_h(0)
        vg.append(late.tile([P, V - HV], U32, name="vg1", offset=3 * V, align_bytes=256))
        nc.vector.tensor_copy(vg[1][:], v_win[:].bitcast(U32).indirect(cand_t[:, HV // 16 :]))
        quantise_h(1)
        quantise_h(2)

        ex = [tile([P, V], F32, f"ex{c}") for c in range(n_ch)]
        total = [keep.tile([P, 1], F32, name=f"total{c}", tag=f"total{c % 2 if c < 3 else c}", align_bytes=64) for c in range(n_ch)]
        inv = [tile([P, 1], F32, f"inv{c}") for c in range(n_ch)]

        def logits(c):
            hc, hs = hq[c]
            for words, lo, hi in ((vg[0][:, 0:256], 0, 256), (vg[0][:, 256:], 256, HV), (vg[1][:], HV, V)):
                nc.tensor.matmul_mx(out=yp[c][:, lo:hi], lhsT=hc.bitcast(FP8X4), lhsT_scale=hs,
                                    rhs=words.bitcast(FP8X4), rhs_scale=vs[:, lo:hi], start=True, stop=True)
            negmax = keep.tile([P, 1], F32, name=f"negmax{c}", tag=f"negmax{c % 3}", align_bytes=64)
            nc.vector.tensor_reduce(negmax[:], yp[c][:], AX.X, ALU.max, negate=True)
            nc.scalar.activation(ex[c][:], yp[c][:], ACT.Exp, bias=negmax[:], scale=1.0, accum_out=total[c][:])

        def invert(c):
            nc.vector.reciprocal(inv[c][:], total[c][:])

        def finish(c):
            res = tile([P, V], F32, f"res{c}")
            nc.vector.tensor_scalar(res[:], ex[c][:], inv[c][:], None, ALU.mult)
            nc.sync.dma_start(out[c * CH : (c + 1) * CH, :], res[:])

        logits(0)
        quantise_h(3)
        logits(1)
        invert(0)
        res_first = tile([P, V], F32, "res_first")
        nc.scalar.activation(res_first[:, 0:FIRST], ex[0][:, 0:FIRST], ACT.Copy, scale=inv[0][:])
        nc.sync.dma_start(out[0:CH, 0:FIRST], res_first[:, 0:FIRST])
        logits(2)
        logits(3)
        nc.vector.tensor_scalar(res_first[:, FIRST:], ex[0][:, FIRST:], inv[0][:], None, ALU.mult)
        nc.sync.dma_start(out[0:CH, FIRST:], res_first[:, FIRST:])
        invert(1)
        invert(2)
        finish(1)
        finish(2)
        invert(3)
        res_last = tile([P, V], F32, "res_last")
        nc.vector.tensor_scalar(res_last[:, 0:320], ex[3][:, 0:320], inv[3][:], None, ALU.mult)
        nc.scalar.activation(res_last[:, 320:], ex[3][:, 320:], ACT.Copy, scale=inv[3][:])
        nc.sync.dma_start(out[3 * CH :, :], res_last[:])
